import numpy as np
CORES = [16,20,17,21,18,22,19,23,24,28,25,29,26,30,27,31]
N = 16
def setup_inputs(rng):
    return {"x": rng.standard_normal((N, 128, 1024), dtype=np.float32)}
def reference(x):
    g = np.concatenate(list(x), axis=1)
    return {"y": np.broadcast_to(g, (N,) + g.shape)}

@@ -1,0 +1,94 @@
+import concourse.bass as bass
+SCRATCH = {'land': ('sbuf', [128, 16384], 'float32')}
+SEMAPHORES = ['ld', 'st', 'sent', 'xa', 'xb', 'pa', 'pb', 'on', 'f0', 'f1', 'f2', 'f3']
+RELAY_SRC = {2: 0, 3: 1, 6: 4, 7: 5}
+
+def rank_program(g, core, T, topo):
+    s = T.sem
+    ch, k = (topo.chip(core), core % 8)
+    rank = T.rank_of(core)
+
+    def blk(r):
+        return T.land[:, r * 1024:(r + 1) * 1024]
+
+    def half(r, h):
+        return T.land[:, r * 1024 + h * 512:r * 1024 + (h + 1) * 512]
+
+    def send(dst, ap, sem):
+        a = topo.addr(dst)
+        g.remote_dma(ap, ap, remote_sem=sem, local_sem=s.sent, pid=a[1], routing_id=a[0], dma_engine_mask=255)
+
+    def fan(dsts, ap, sem):
+        ids = [bass.DstId(rid=topo.addr(d)[0], pnc=topo.addr(d)[1]) for d in dsts]
+        g.remote_dma_fused([bass.RemoteDMATransfer(dst_ids=ids, dma_engine_mask=65535, remote_sem=sem, srcs=[ap], dsts=[ap] * len(dsts))], local_sem=s.sent)
+    if rank is None:
+        if k in RELAY_SRC:
+            r = T.rank_of((ch + 2) * 8 + RELAY_SRC[k])
+            dst = (ch + 2 ^ 1) * 8 + RELAY_SRC[k]
+            g.wait_ge(s.xa, 8)
+            send(dst, half(r, 0), s.xa)
+            g.wait_ge(s.xb, 8)
+            send(dst, half(r, 1), s.xb)
+            g.wait_ge(s.sent, 16)
+        return
+    mates = [ch * 8 + k // 4 * 4 + (k + i) % 4 for i in (1, 2, 3)]
+    partner = ch * 8 + (k ^ 4)
+    twin = (ch ^ 1) * 8 + k
+    own_half = rank // 8 * 8192
+    far_half = 8192 - own_half
+    direct = topo.may_write(core, twin)
+    late = k % 2 == 1
+    fs = [s.f0, s.f1, s.f2, s.f3]
+    stores = []
+
+    def store(col, n):
+        g.dma_start(T.y[:, col:col + n], T.land[:, col:col + n]).then_inc(s.st, 16)
+        stores.append(col)
+
+    def cross():
+        if direct:
+            send(twin, blk(rank), s.xa)
+        else:
+            send((ch - 2) * 8 + k + 2, half(rank, 0), s.xa)
+            send((ch - 2) * 8 + k + 2, half(rank, 1), s.xb)
+
+    def store_own_rest(done):
+        g.wait_ge(s.on, 6 * 16)
+        b = 0
+        while b < 8:
+            e = b
+            while e < 8 and e not in done:
+                e += 1
+            if e > b:
+                store(own_half + b * 1024, (e - b) * 1024)
+            b = e + 1
+    g.dma_start(blk(rank), T.x[:, :]).then_inc(s.ld, 16)
+    g.dma_start(T.y[:, rank * 1024:(rank + 1) * 1024], T.x[:, :]).then_inc(s.st, 16)
+    stores.append(rank * 1024)
+    g.wait_ge(s.ld, 16)
+    if not late:
+        cross()
+    fan([partner], blk(rank), s.pa)
+    fan(mates, blk(rank), s.on)
+    if late:
+        cross()
+    g.wait_ge(s.pa, 16)
+    fan(mates, blk(T.rank_of(partner)), s.on)
+    if late and (not direct):
+        store(T.rank_of(partner) * 1024, 1024)
+        store_own_rest([rank % 8, T.rank_of(partner) % 8])
+    g.wait_ge(s.xa, 8)
+    if not direct:
+        g.wait_ge(s.xb, 8)
+    fan([partner], blk(T.rank_of(twin)), s.pb)
+    fan(mates, blk(T.rank_of(twin)), fs[k % 4])
+    g.wait_ge(s.pb, 16)
+    fan(mates, blk(T.rank_of(twin ^ 4)), fs[k % 4])
+    if direct or not late:
+        store_own_rest([rank % 8])
+    for j in (2, 3, 0, 1):
+        if j != k % 4:
+            g.wait_ge(fs[j], 2 * 16)
+        store(far_half + j * 2048, 2048)
+    g.wait_ge(s.st, 16 * len(stores))
+    g.wait_ge(s.sent, (8 if direct else 16) + 6 * 16)

@@ -1,7 +1,8 @@
 import concourse.bass as bass
 SCRATCH = {'land': ('sbuf', [128, 16384], 'float32')}
-SEMAPHORES = ['ld', 'st', 'sent', 'xa', 'xb', 'pa', 'pb', 'on', 'f0', 'f1', 'f2', 'f3']
+SEMAPHORES = ['ld', 'ss', 'sc', 'sent', 'xa', 'xb', 'pa', 'pb', 'on', 'f0', 'f1', 'f2', 'f3']
 RELAY_SRC = {2: 0, 3: 1, 6: 4, 7: 5}
+
 
 def rank_program(g, core, T, topo):
     s = T.sem
@@ -39,11 +40,6 @@ def rank_program(g, core, T, topo):
     direct = topo.may_write(core, twin)
     late = k % 2 == 1
     fs = [s.f0, s.f1, s.f2, s.f3]
-    stores = []
-
-    def store(col, n):
-        g.dma_start(T.y[:, col:col + n], T.land[:, col:col + n]).then_inc(s.st, 16)
-        stores.append(col)
 
     def cross():
         if direct:
@@ -52,19 +48,9 @@ def rank_program(g, core, T, topo):
             send((ch - 2) * 8 + k + 2, half(rank, 0), s.xa)
             send((ch - 2) * 8 + k + 2, half(rank, 1), s.xb)
 
-    def store_own_rest(done):
-        g.wait_ge(s.on, 6 * 16)
-        b = 0
-        while b < 8:
-            e = b
-            while e < 8 and e not in done:
-                e += 1
-            if e > b:
-                store(own_half + b * 1024, (e - b) * 1024)
-            b = e + 1
-    g.dma_start(blk(rank), T.x[:, :]).then_inc(s.ld, 16)
-    g.dma_start(T.y[:, rank * 1024:(rank + 1) * 1024], T.x[:, :]).then_inc(s.st, 16)
-    stores.append(rank * 1024)
+    g.sync.dma_start(blk(rank), T.x[:, :]).then_inc(s.ld, 16)
+    g.scalar.dma_start(T.y[:, rank * 1024:(rank + 1) * 1024], T.x[:, :]).then_inc(s.sc, 16)
+
     g.wait_ge(s.ld, 16)
     if not late:
         cross()
@@ -74,9 +60,6 @@ def rank_program(g, core, T, topo):
         cross()
     g.wait_ge(s.pa, 16)
     fan(mates, blk(T.rank_of(partner)), s.on)
-    if late and (not direct):
-        store(T.rank_of(partner) * 1024, 1024)
-        store_own_rest([rank % 8, T.rank_of(partner) % 8])
     g.wait_ge(s.xa, 8)
     if not direct:
         g.wait_ge(s.xb, 8)
@@ -84,11 +67,27 @@ def rank_program(g, core, T, topo):
     fan(mates, blk(T.rank_of(twin)), fs[k % 4])
     g.wait_ge(s.pb, 16)
     fan(mates, blk(T.rank_of(twin ^ 4)), fs[k % 4])
-    if direct or not late:
-        store_own_rest([rank % 8])
-    for j in (2, 3, 0, 1):
-        if j != k % 4:
-            g.wait_ge(fs[j], 2 * 16)
-        store(far_half + j * 2048, 2048)
-    g.wait_ge(s.st, 16 * len(stores))
     g.wait_ge(s.sent, (8 if direct else 16) + 6 * 16)
+
+    jobs = []
+    ow = [(s.pa, 16), (s.on, 96)]
+    o = rank % 8
+    if o > 0:
+        jobs.append((own_half, o * 1024, ow))
+    if o < 7:
+        jobs.append((own_half + (o + 1) * 1024, (7 - o) * 1024, ow))
+    if len(jobs) == 1:
+        c, n, w = jobs[0]
+        jobs = [(c, 4096, w), (c + 4096, n - 4096, w)]
+    for j in (2, 3, 0, 1):
+        if j == k % 4:
+            w = [(s.xa, 8), (s.pb, 16)] + ([] if direct else [(s.xb, 8)])
+        else:
+            w = [(fs[j], 32)]
+        jobs.append((far_half + j * 2048, 2048, w))
+    for q, sm, mine, base in ((g.sync, s.ss, jobs[0::2], 0), (g.scalar, s.sc, jobs[1::2], 1)):
+        for c, n, w in mine:
+            for a, v in w:
+                q.wait_ge(a, v)
+            q.dma_start(T.y[:, c:c + n], T.land[:, c:c + n]).then_inc(sm, 16)
+        q.wait_ge(sm, 16 * (len(mine) + base))

@@ -2,6 +2,7 @@ import concourse.bass as bass
 SCRATCH = {'land': ('sbuf', [128, 16384], 'float32')}
 SEMAPHORES = ['ld', 'ss', 'sc', 'sent', 'xa', 'xb', 'pa', 'pb', 'on', 'f0', 'f1', 'f2', 'f3']
 RELAY_SRC = {2: 0, 3: 1, 6: 4, 7: 5}
+XM, NX = 0x000F, 4
 
 
 def rank_program(g, core, T, topo):
@@ -15,21 +16,39 @@ def rank_program(g, core, T, topo):
     def half(r, h):
         return T.land[:, r * 1024 + h * 512:r * 1024 + (h + 1) * 512]
 
-    def send(dst, ap, sem):
+    sent = [0]
+
+    def send(dst, ap, sem, mask, n):
         a = topo.addr(dst)
-        g.remote_dma(ap, ap, remote_sem=sem, local_sem=s.sent, pid=a[1], routing_id=a[0], dma_engine_mask=255)
+        g.remote_dma(ap, ap, remote_sem=sem, local_sem=s.sent, pid=a[1], routing_id=a[0], dma_engine_mask=mask)
+        sent[0] += n
+
+    def ids(dsts):
+        return [bass.DstId(rid=topo.addr(d)[0], pnc=topo.addr(d)[1]) for d in dsts]
+
+    def one(dst, ap, sem):
+        g.remote_dma_fused([bass.RemoteDMATransfer(dst_ids=ids([dst]), dma_engine_mask=0xFF00, remote_sem=sem, srcs=[ap], dsts=[ap])], local_sem=s.sent)
+        sent[0] += 8
+
+    def fan3(dsts, ap, sem):
+        g.remote_dma_fused([
+            bass.RemoteDMATransfer(dst_ids=ids(dsts[:2]), dma_engine_mask=0xFF00, remote_sem=sem, srcs=[ap], dsts=[ap] * 2),
+            bass.RemoteDMATransfer(dst_ids=ids(dsts[2:]), dma_engine_mask=0x00F0, remote_sem=sem, srcs=[ap], dsts=[ap])],
+            local_sem=s.sent)
+        sent[0] += 12
 
     def fan(dsts, ap, sem):
-        ids = [bass.DstId(rid=topo.addr(d)[0], pnc=topo.addr(d)[1]) for d in dsts]
-        g.remote_dma_fused([bass.RemoteDMATransfer(dst_ids=ids, dma_engine_mask=65535, remote_sem=sem, srcs=[ap], dsts=[ap] * len(dsts))], local_sem=s.sent)
+        g.remote_dma_fused([bass.RemoteDMATransfer(dst_ids=ids(dsts), dma_engine_mask=0xFFFF, remote_sem=sem, srcs=[ap], dsts=[ap] * len(dsts))], local_sem=s.sent)
+        sent[0] += 16
+
     if rank is None:
         if k in RELAY_SRC:
             r = T.rank_of((ch + 2) * 8 + RELAY_SRC[k])
             dst = (ch + 2 ^ 1) * 8 + RELAY_SRC[k]
-            g.wait_ge(s.xa, 8)
-            send(dst, half(r, 0), s.xa)
-            g.wait_ge(s.xb, 8)
-            send(dst, half(r, 1), s.xb)
+            g.wait_ge(s.xa, NX)
+            send(dst, half(r, 0), s.xa, 255, 8)
+            g.wait_ge(s.xb, NX)
+            send(dst, half(r, 1), s.xb, 255, 8)
             g.wait_ge(s.sent, 16)
         return
     mates = [ch * 8 + k // 4 * 4 + (k + i) % 4 for i in (1, 2, 3)]
@@ -40,13 +59,17 @@ def rank_program(g, core, T, topo):
     direct = topo.may_write(core, twin)
     late = k % 2 == 1
     fs = [s.f0, s.f1, s.f2, s.f3]
+    nin = NX if direct else 8
+
+    def got(j):
+        return 2 * (4 if (k - j) % 4 == 3 else 8)
 
     def cross():
         if direct:
-            send(twin, blk(rank), s.xa)
+            send(twin, blk(rank), s.xa, XM, NX)
         else:
-            send((ch - 2) * 8 + k + 2, half(rank, 0), s.xa)
-            send((ch - 2) * 8 + k + 2, half(rank, 1), s.xb)
+            send((ch - 2) * 8 + k + 2, half(rank, 0), s.xa, XM, NX)
+            send((ch - 2) * 8 + k + 2, half(rank, 1), s.xb, XM, NX)
 
     g.sync.dma_start(blk(rank), T.x[:, :]).then_inc(s.ld, 16)
     g.scalar.dma_start(T.y[:, rank * 1024:(rank + 1) * 1024], T.x[:, :]).then_inc(s.sc, 16)
@@ -54,23 +77,23 @@ def rank_program(g, core, T, topo):
     g.wait_ge(s.ld, 16)
     if not late:
         cross()
-    fan([partner], blk(rank), s.pa)
-    fan(mates, blk(rank), s.on)
+    one(partner, blk(rank), s.pa)
+    fan3(mates, blk(rank), s.on)
     if late:
         cross()
-    g.wait_ge(s.pa, 16)
-    fan(mates, blk(T.rank_of(partner)), s.on)
-    g.wait_ge(s.xa, 8)
+    g.wait_ge(s.pa, 8)
+    fan3(mates, blk(T.rank_of(partner)), s.on)
+    g.wait_ge(s.xa, nin)
     if not direct:
-        g.wait_ge(s.xb, 8)
+        g.wait_ge(s.xb, nin)
     fan([partner], blk(T.rank_of(twin)), s.pb)
     fan(mates, blk(T.rank_of(twin)), fs[k % 4])
     g.wait_ge(s.pb, 16)
     fan(mates, blk(T.rank_of(twin ^ 4)), fs[k % 4])
-    g.wait_ge(s.sent, (8 if direct else 16) + 6 * 16)
+    g.wait_ge(s.sent, sent[0])
 
     jobs = []
-    ow = [(s.pa, 16), (s.on, 96)]
+    ow = [(s.pa, 8), (s.on, sum(got(j) for j in range(4) if j != k % 4))]
     o = rank % 8
     if o > 0:
         jobs.append((own_half, o * 1024, ow))
@@ -81,7 +104,7 @@ def rank_program(g, core, T, topo):
         jobs = [(c, 4096, w), (c + 4096, n - 4096, w)]
     for j in (2, 3, 0, 1):
         if j == k % 4:
-            w = [(s.xa, 8), (s.pb, 16)] + ([] if direct else [(s.xb, 8)])
+            w = [(s.xa, nin), (s.pb, 16)] + ([] if direct else [(s.xb, nin)])
         else:
             w = [(fs[j], 32)]
         jobs.append((far_half + j * 2048, 2048, w))

@@ -1,6 +1,6 @@
 import concourse.bass as bass
 SCRATCH = {'land': ('sbuf', [128, 16384], 'float32')}
-SEMAPHORES = ['ld', 'ss', 'sc', 'sent', 'xa', 'xb', 'pa', 'pb', 'on', 'f0', 'f1', 'f2', 'f3']
+SEMAPHORES = ['ld', 'ss', 'sc', 'sent', 'xa', 'xb', 'pa', 'pb', 'on', 'nb', 'f0', 'f1', 'f2', 'f3']
 RELAY_SRC = {2: 0, 3: 1, 6: 4, 7: 5}
 XM, NX = 0x000F, 4
 
@@ -23,23 +23,13 @@ def rank_program(g, core, T, topo):
         g.remote_dma(ap, ap, remote_sem=sem, local_sem=s.sent, pid=a[1], routing_id=a[0], dma_engine_mask=mask)
         sent[0] += n
 
-    def ids(dsts):
-        return [bass.DstId(rid=topo.addr(d)[0], pnc=topo.addr(d)[1]) for d in dsts]
-
-    def one(dst, ap, sem):
-        g.remote_dma_fused([bass.RemoteDMATransfer(dst_ids=ids([dst]), dma_engine_mask=0xFF00, remote_sem=sem, srcs=[ap], dsts=[ap])], local_sem=s.sent)
-        sent[0] += 8
-
-    def fan3(dsts, ap, sem):
-        g.remote_dma_fused([
-            bass.RemoteDMATransfer(dst_ids=ids(dsts[:2]), dma_engine_mask=0xFF00, remote_sem=sem, srcs=[ap], dsts=[ap] * 2),
-            bass.RemoteDMATransfer(dst_ids=ids(dsts[2:]), dma_engine_mask=0x00F0, remote_sem=sem, srcs=[ap], dsts=[ap])],
-            local_sem=s.sent)
-        sent[0] += 12
-
-    def fan(dsts, ap, sem):
-        g.remote_dma_fused([bass.RemoteDMATransfer(dst_ids=ids(dsts), dma_engine_mask=0xFFFF, remote_sem=sem, srcs=[ap], dsts=[ap] * len(dsts))], local_sem=s.sent)
-        sent[0] += 16
+    def call(ap, *parts):
+        trs = []
+        for dsts, mask, sem in parts:
+            ids = [bass.DstId(rid=topo.addr(d)[0], pnc=topo.addr(d)[1]) for d in dsts]
+            trs.append(bass.RemoteDMATransfer(dst_ids=ids, dma_engine_mask=mask, remote_sem=sem, srcs=[ap], dsts=[ap] * len(dsts)))
+            sent[0] += bin(mask).count('1')
+        g.remote_dma_fused(trs, local_sem=s.sent)
 
     if rank is None:
         if k in RELAY_SRC:
@@ -51,49 +41,67 @@ def rank_program(g, core, T, topo):
             send(dst, half(r, 1), s.xb, 255, 8)
             g.wait_ge(s.sent, 16)
         return
+    k4 = k % 4
     mates = [ch * 8 + k // 4 * 4 + (k + i) % 4 for i in (1, 2, 3)]
     partner = ch * 8 + (k ^ 4)
     twin = (ch ^ 1) * 8 + k
     own_half = rank // 8 * 8192
     far_half = 8192 - own_half
     direct = topo.may_write(core, twin)
-    late = k % 2 == 1
+    port = k % 2 == 0
     fs = [s.f0, s.f1, s.f2, s.f3]
     nin = NX if direct else 8
 
-    def got(j):
-        return 2 * (4 if (k - j) % 4 == 3 else 8)
-
-    def cross():
+    def cross(c):
+        r = T.rank_of(c)
         if direct:
-            send(twin, blk(rank), s.xa, XM, NX)
+            send(c ^ 8, blk(r), s.xa, XM, NX)
         else:
-            send((ch - 2) * 8 + k + 2, half(rank, 0), s.xa, XM, NX)
-            send((ch - 2) * 8 + k + 2, half(rank, 1), s.xb, XM, NX)
+            send(c - 16 + 2, half(r, 0), s.xa, XM, NX)
+            send(c - 16 + 2, half(r, 1), s.xb, XM, NX)
+
+    def to_partner(ap, sem):
+        call(ap, ([partner], 0xFF00 if port else 0xFFFF, sem))
+
+    def to_mates(ap, sem):
+        if port:
+            call(ap, (mates[:2], 0xFF00, sem), (mates[2:], 0x00F0, sem))
+        else:
+            call(ap, (mates, 0xFFFF, sem))
+
+    def e(j):
+        if j % 2 == 1:
+            return 16
+        return 4 if (k4 - j) % 4 == 3 else 8
 
     g.sync.dma_start(blk(rank), T.x[:, :]).then_inc(s.ld, 16)
     g.scalar.dma_start(T.y[:, rank * 1024:(rank + 1) * 1024], T.x[:, :]).then_inc(s.sc, 16)
 
     g.wait_ge(s.ld, 16)
-    if not late:
-        cross()
-    one(partner, blk(rank), s.pa)
-    fan3(mates, blk(rank), s.on)
-    if late:
-        cross()
+    if port:
+        cross(core)
+        call(blk(rank), ([partner], 0xFF00, s.pa))
+        to_mates(blk(rank), s.on)
+        g.wait_ge(s.nb, 8)
+        cross(core + 1)
+    else:
+        call(blk(rank), ([core - 1], 0x00FF, s.nb), ([partner], 0xFF00, s.pa))
+        call(blk(rank), (mates[:2], 0xFFFF, s.on))
     g.wait_ge(s.pa, 8)
-    fan3(mates, blk(T.rank_of(partner)), s.on)
+    to_mates(blk(T.rank_of(partner)), s.on)
     g.wait_ge(s.xa, nin)
     if not direct:
         g.wait_ge(s.xb, nin)
-    fan([partner], blk(T.rank_of(twin)), s.pb)
-    fan(mates, blk(T.rank_of(twin)), fs[k % 4])
-    g.wait_ge(s.pb, 16)
-    fan(mates, blk(T.rank_of(twin ^ 4)), fs[k % 4])
+    npb = 8 if port else 16
+    to_partner(blk(T.rank_of(twin)), s.pb)
+    to_mates(blk(T.rank_of(twin)), fs[k4])
+    g.wait_ge(s.pb, npb)
+    to_mates(blk(T.rank_of(twin ^ 4)), fs[k4])
     g.wait_ge(s.sent, sent[0])
 
     jobs = []
-    ow = [(s.pa, 8), (s.on, sum(got(j) for j in range(4) if j != k % 4))]
+    non = sum(2 * e(j) for j in range(4) if j != k4) - (16 if port else 0)
+    ow = [(s.pa, 8), (s.on, non)] + ([(s.nb, 8)] if port else [])
     o = rank % 8
     if o > 0:
         jobs.append((own_half, o * 1024, ow))
@@ -102,11 +110,11 @@ def rank_program(g, core, T, topo):
     if len(jobs) == 1:
         c, n, w = jobs[0]
         jobs = [(c, 4096, w), (c + 4096, n - 4096, w)]
-    for j in (2, 3, 0, 1):
-        if j == k % 4:
-            w = [(s.xa, nin), (s.pb, 16)] + ([] if direct else [(s.xb, nin)])
+    for j in (2, 0, 3, 1):
+        if j == k4:
+            w = [(s.xa, nin), (s.pb, npb)] + ([] if direct else [(s.xb, nin)])
         else:
-            w = [(fs[j], 32)]
+            w = [(fs[j], 2 * e(j))]
         jobs.append((far_half + j * 2048, 2048, w))
     for q, sm, mine, base in ((g.sync, s.ss, jobs[0::2], 0), (g.scalar, s.sc, jobs[1::2], 1)):
         for c, n, w in mine:

@@ -1,6 +1,7 @@
 import concourse.bass as bass
 SCRATCH = {'land': ('sbuf', [128, 16384], 'float32')}
-SEMAPHORES = ['ld', 'ss', 'sc', 'sent', 'xa', 'xb', 'pa', 'pb', 'on', 'nb', 'f0', 'f1', 'f2', 'f3']
+SEMAPHORES = ['ld', 'ss', 'sc', 'sent', 'xa', 'xb', 'pa', 'pb', 'nb', 'f0', 'f1', 'f2', 'f3',
+              'na0', 'na1', 'na2', 'na3', 'nc0', 'nc1', 'nc2', 'nc3']
 RELAY_SRC = {2: 0, 3: 1, 6: 4, 7: 5}
 XM, NX = 0x000F, 4
 
@@ -42,14 +43,16 @@ def rank_program(g, core, T, topo):
             g.wait_ge(s.sent, 16)
         return
     k4 = k % 4
-    mates = [ch * 8 + k // 4 * 4 + (k + i) % 4 for i in (1, 2, 3)]
+    die0 = ch * 8 + k // 4 * 4
+    mates = [die0 + (k + i) % 4 for i in (1, 2, 3)]
     partner = ch * 8 + (k ^ 4)
     twin = (ch ^ 1) * 8 + k
-    own_half = rank // 8 * 8192
-    far_half = 8192 - own_half
+    far_half = 8192 - rank // 8 * 8192
     direct = topo.may_write(core, twin)
     port = k % 2 == 0
     fs = [s.f0, s.f1, s.f2, s.f3]
+    na = [s.na0, s.na1, s.na2, s.na3]
+    nc = [s.nc0, s.nc1, s.nc2, s.nc3]
     nin = NX if direct else 8
 
     def cross(c):
@@ -81,17 +84,17 @@ def rank_program(g, core, T, topo):
     if port:
         cross(core)
         call(blk(rank), ([partner], 0xFF00, s.pa))
-        to_mates(blk(rank), s.on)
+        to_mates(blk(rank), na[k4])
         g.wait_ge(s.nb, 8)
         cross(core + 1)
     else:
         call(blk(rank), ([core - 1], 0x00FF, s.nb), ([partner], 0xFF00, s.pa))
-        call(blk(rank), (mates[:2], 0xFFFF, s.on))
+        call(blk(rank), (mates[:2], 0xFFFF, na[k4]))
     g.wait_ge(s.pa, 8)
-    to_mates(blk(T.rank_of(partner)), s.on)
-    g.wait_ge(s.xa, nin)
-    if not direct:
-        g.wait_ge(s.xb, nin)
+    to_mates(blk(T.rank_of(partner)), nc[k4])
+    xw = [(s.xa, nin)] + ([] if direct else [(s.xb, nin)])
+    for a, v in xw:
+        g.wait_ge(a, v)
     npb = 8 if port else 16
     to_partner(blk(T.rank_of(twin)), s.pb)
     to_mates(blk(T.rank_of(twin)), fs[k4])
@@ -99,20 +102,17 @@ def rank_program(g, core, T, topo):
     to_mates(blk(T.rank_of(twin ^ 4)), fs[k4])
     g.wait_ge(s.sent, sent[0])
 
-    jobs = []
-    non = sum(2 * e(j) for j in range(4) if j != k4) - (16 if port else 0)
-    ow = [(s.pa, 8), (s.on, non)] + ([(s.nb, 8)] if port else [])
-    o = rank % 8
-    if o > 0:
-        jobs.append((own_half, o * 1024, ow))
-    if o < 7:
-        jobs.append((own_half + (o + 1) * 1024, (7 - o) * 1024, ow))
-    if len(jobs) == 1:
-        c, n, w = jobs[0]
-        jobs = [(c, 4096, w), (c + 4096, n - 4096, w)]
+    jobs = [(T.rank_of(partner) * 1024, 1024, [(s.pa, 8)])]
+    for i in (3, 2, 1):
+        j = (k4 + i) % 4
+        w = [(s.nb, 8)] if port and i == 1 else [(na[j], e(j))]
+        jobs.append((T.rank_of(die0 + j) * 1024, 1024, w))
+    for i in (3, 2, 1):
+        j = (k4 + i) % 4
+        jobs.append((T.rank_of((die0 + j) ^ 4) * 1024, 1024, [(nc[j], e(j))]))
     for j in (2, 0, 3, 1):
         if j == k4:
-            w = [(s.xa, nin), (s.pb, npb)] + ([] if direct else [(s.xb, nin)])
+            w = xw + [(s.pb, npb)]
         else:
             w = [(fs[j], 2 * e(j))]
         jobs.append((far_half + j * 2048, 2048, w))

@@ -1,6 +1,6 @@
 import concourse.bass as bass
 SCRATCH = {'land': ('sbuf', [128, 16384], 'float32')}
-SEMAPHORES = ['ld', 'ss', 'sc', 'sent', 'xa', 'xb', 'pa', 'pb', 'nb', 'f0', 'f1', 'f2', 'f3',
+SEMAPHORES = ['ld', 'ss', 'sc', 'sent', 'xa', 'xb', 'xc', 'xd', 'pa', 'pb', 'nb', 'f0', 'f1', 'f2', 'f3',
               'na0', 'na1', 'na2', 'na3', 'nc0', 'nc1', 'nc2', 'nc3']
 RELAY_SRC = {2: 0, 3: 1, 6: 4, 7: 5}
 XM, NX = 0x000F, 4
@@ -14,9 +14,10 @@ def rank_program(g, core, T, topo):
     def blk(r):
         return T.land[:, r * 1024:(r + 1) * 1024]
 
-    def half(r, h):
-        return T.land[:, r * 1024 + h * 512:r * 1024 + (h + 1) * 512]
+    def quarter(r, h):
+        return T.land[:, r * 1024 + h * 256:r * 1024 + (h + 1) * 256]
 
+    xq = [s.xa, s.xb, s.xc, s.xd]
     sent = [0]
 
     def send(dst, ap, sem, mask, n):
@@ -36,11 +37,10 @@ def rank_program(g, core, T, topo):
         if k in RELAY_SRC:
             r = T.rank_of((ch + 2) * 8 + RELAY_SRC[k])
             dst = (ch + 2 ^ 1) * 8 + RELAY_SRC[k]
-            g.wait_ge(s.xa, NX)
-            send(dst, half(r, 0), s.xa, 255, 8)
-            g.wait_ge(s.xb, NX)
-            send(dst, half(r, 1), s.xb, 255, 8)
-            g.wait_ge(s.sent, 16)
+            for h in range(4):
+                g.wait_ge(xq[h], NX)
+                send(dst, quarter(r, h), xq[h], 255, 8)
+            g.wait_ge(s.sent, 32)
         return
     k4 = k % 4
     die0 = ch * 8 + k // 4 * 4
@@ -55,13 +55,14 @@ def rank_program(g, core, T, topo):
     nc = [s.nc0, s.nc1, s.nc2, s.nc3]
     nin = NX if direct else 8
 
-    def cross(c):
+    def cross(c, hs):
         r = T.rank_of(c)
         if direct:
-            send(c ^ 8, blk(r), s.xa, XM, NX)
+            if 0 in hs:
+                send(c ^ 8, blk(r), s.xa, XM, NX)
         else:
-            send(c - 16 + 2, half(r, 0), s.xa, XM, NX)
-            send(c - 16 + 2, half(r, 1), s.xb, XM, NX)
+            for h in hs:
+                send(c - 16 + 2, quarter(r, h), xq[h], XM, NX)
 
     def to_partner(ap, sem):
         call(ap, ([partner], 0xFF00 if port else 0xFFFF, sem))
@@ -82,17 +83,19 @@ def rank_program(g, core, T, topo):
 
     g.wait_ge(s.ld, 16)
     if port:
-        cross(core)
+        cross(core, [0])
         call(blk(rank), ([partner], 0xFF00, s.pa))
+        cross(core, [1])
         to_mates(blk(rank), na[k4])
+        cross(core, [2, 3])
         g.wait_ge(s.nb, 8)
-        cross(core + 1)
+        cross(core + 1, [0, 1, 2, 3])
     else:
         call(blk(rank), ([core - 1], 0x00FF, s.nb), ([partner], 0xFF00, s.pa))
         call(blk(rank), (mates[:2], 0xFFFF, na[k4]))
     g.wait_ge(s.pa, 8)
     to_mates(blk(T.rank_of(partner)), nc[k4])
-    xw = [(s.xa, nin)] + ([] if direct else [(s.xb, nin)])
+    xw = [(s.xa, nin)] if direct else [(q, nin) for q in xq]
     for a, v in xw:
         g.wait_ge(a, v)
     npb = 8 if port else 16

import concourse.bass as bass
SCRATCH = {'land': ('sbuf', [128, 16384], 'float32')}
SEMAPHORES = ['ld', 'ss', 'sc', 'sent', 'xa', 'xb', 'xc', 'xd', 'pa', 'pb', 'nb', 'f0', 'f1', 'f2', 'f3',
              'na0', 'na1', 'na2', 'na3', 'nc0', 'nc1', 'nc2', 'nc3']
RELAY_SRC = {2: 0, 3: 1, 6: 4, 7: 5}
XM, NX = 0x000F, 4


def rank_program(g, core, T, topo):
    s = T.sem
    ch, k = (topo.chip(core), core % 8)
    rank = T.rank_of(core)

    def blk(r):
        return T.land[:, r * 1024:(r + 1) * 1024]

    def quarter(r, h):
        return T.land[:, r * 1024 + h * 256:r * 1024 + (h + 1) * 256]

    xq = [s.xa, s.xb, s.xc, s.xd]
    sent = [0]

    def send(dst, ap, sem, mask, n):
        a = topo.addr(dst)
        g.remote_dma(ap, ap, remote_sem=sem, local_sem=s.sent, pid=a[1], routing_id=a[0], dma_engine_mask=mask)
        sent[0] += n

    def call(ap, *parts):
        trs = []
        for dsts, mask, sem in parts:
            ids = [bass.DstId(rid=topo.addr(d)[0], pnc=topo.addr(d)[1]) for d in dsts]
            trs.append(bass.RemoteDMATransfer(dst_ids=ids, dma_engine_mask=mask, remote_sem=sem, srcs=[ap], dsts=[ap] * len(dsts)))
            sent[0] += bin(mask).count('1')
        g.remote_dma_fused(trs, local_sem=s.sent)

    if rank is None:
        if k in RELAY_SRC:
            r = T.rank_of((ch + 2) * 8 + RELAY_SRC[k])
            dst = (ch + 2 ^ 1) * 8 + RELAY_SRC[k]
            for h in range(4):
                g.wait_ge(xq[h], NX)
                send(dst, quarter(r, h), xq[h], 255, 8)
            g.wait_ge(s.sent, 32)
        return
    k4 = k % 4
    die0 = ch * 8 + k // 4 * 4
    mates = [die0 + (k + i) % 4 for i in (1, 2, 3)]
    partner = ch * 8 + (k ^ 4)
    twin = (ch ^ 1) * 8 + k
    far_half = 8192 - rank // 8 * 8192
    direct = topo.may_write(core, twin)
    port = k % 2 == 0
    fs = [s.f0, s.f1, s.f2, s.f3]
    na = [s.na0, s.na1, s.na2, s.na3]
    nc = [s.nc0, s.nc1, s.nc2, s.nc3]
    nin = NX if direct else 8

    def cross(c, hs):
        r = T.rank_of(c)
        if direct:
            if 0 in hs:
                send(c ^ 8, blk(r), s.xa, XM, NX)
        else:
            for h in hs:
                send(c - 16 + 2, quarter(r, h), xq[h], XM, NX)

    def to_partner(ap, sem):
        call(ap, ([partner], 0xFF00 if port else 0xFFFF, sem))

    def to_mates(ap, sem):
        if port:
            call(ap, (mates[:2], 0xFF00, sem), (mates[2:], 0x00F0, sem))
        else:
            call(ap, (mates, 0xFFFF, sem))

    def e(j):
        if j % 2 == 1:
            return 16
        return 4 if (k4 - j) % 4 == 3 else 8

    g.sync.dma_start(blk(rank), T.x[:, :]).then_inc(s.ld, 16)
    g.scalar.dma_start(T.y[:, rank * 1024:(rank + 1) * 1024], T.x[:, :]).then_inc(s.sc, 16)

    g.wait_ge(s.ld, 16)
    if port:
        cross(core, [0])
        call(blk(rank), ([partner], 0xFF00, s.pa))
        cross(core, [1])
        to_mates(blk(rank), na[k4])
        cross(core, [2, 3])
        g.wait_ge(s.nb, 8)
        cross(core + 1, [0, 1, 2, 3])
    else:
        call(blk(rank), ([core - 1], 0x00FF, s.nb), ([partner], 0xFF00, s.pa))
        call(blk(rank), (mates[:2], 0xFFFF, na[k4]))
    g.wait_ge(s.pa, 8)
    to_mates(blk(T.rank_of(partner)), nc[k4])
    xw = [(s.xa, nin)] if direct else [(q, nin) for q in xq]
    for a, v in xw:
        g.wait_ge(a, v)
    npb = 8 if port else 16
    to_partner(blk(T.rank_of(twin)), s.pb)
    to_mates(blk(T.rank_of(twin)), fs[k4])
    g.wait_ge(s.pb, npb)
    to_mates(blk(T.rank_of(twin ^ 4)), fs[k4])
    g.wait_ge(s.sent, sent[0])

    jobs = [(T.rank_of(partner) * 1024, 1024, [(s.pa, 8)])]
    for i in (3, 2, 1):
        j = (k4 + i) % 4
        w = [(s.nb, 8)] if port and i == 1 else [(na[j], e(j))]
        jobs.append((T.rank_of(die0 + j) * 1024, 1024, w))
    for i in (3, 2, 1):
        j = (k4 + i) % 4
        jobs.append((T.rank_of((die0 + j) ^ 4) * 1024, 1024, [(nc[j], e(j))]))
    for j in (2, 0, 3, 1):
        if j == k4:
            w = xw + [(s.pb, npb)]
        else:
            w = [(fs[j], 2 * e(j))]
        jobs.append((far_half + j * 2048, 2048, w))
    for q, sm, mine, base in ((g.sync, s.ss, jobs[0::2], 0), (g.scalar, s.sc, jobs[1::2], 1)):
        for c, n, w in mine:
            for a, v in w:
                q.wait_ge(a, v)
            q.dma_start(T.y[:, c:c + n], T.land[:, c:c + n]).then_inc(sm, 16)
        q.wait_ge(sm, 16 * (len(mine) + base))
